import numpy as np
import ml_dtypes


def mxq(x, axis, fmt="e4m3"):
    dtype, down = {"e4m3": (ml_dtypes.float8_e4m3fn, 7), "e5m2": (ml_dtypes.float8_e5m2, 14)}[fmt]
    v = np.moveaxis(np.asarray(x, np.float32).astype(ml_dtypes.bfloat16).astype(np.float64), axis, -1)
    blocks = v.reshape(v.shape[:-1] + (-1, 32))
    amax = np.abs(blocks).max(-1, keepdims=True)
    byte = np.maximum(np.where(amax > 0, np.frexp(amax)[1] - 1 + 127, 0) - down, 1)
    scale = np.exp2(byte - 127.0)
    codes = (blocks / scale).astype(np.float32).astype(dtype).astype(np.float64)
    return np.moveaxis((codes * scale).reshape(v.shape), -1, axis)


WIDE = False


def mx_kscale(k):
    if not WIDE:
        return np.ones(k)
    levels = np.array([30, -30])
    if k % 512:
        return np.exp2(np.random.permutation(np.resize(levels, k // 32))).repeat(32)
    a = np.empty((k // 512, 16))
    for p in range(k // 512):
        a[p, :8] = np.random.permutation(np.resize(levels, 8))
        for g in range(8):
            far = levels[np.abs(levels - a[p, g]) >= 10]
            a[p, g + 8] = far[np.random.randint(len(far))]
    return np.exp2(a.ravel()).repeat(32)


def f64(x):
    return np.asarray(x).astype(np.float64)


def striped(idx):
    return np.tile(np.asarray(idx).reshape(-1, 16).T, (8, 1)).astype(np.uint16)


def unstriped(offs):
    return offs[:16].T.reshape(-1).astype(np.int64)


E2M1 = np.array([0.0, 0.5, 1.0, 1.5, 2.0, 3.0, 4.0, 6.0, -0.0, -0.5, -1.0, -1.5, -2.0, -3.0, -4.0, -6.0])


def pack_weight(w, fmt):
    k, n = w.shape
    w = f64(np.asarray(w, np.float32).astype(ml_dtypes.bfloat16)).reshape(k // 32, 32, n)
    amax = np.abs(w).max(1)
    if fmt in ("e4m3", "e5m2"):
        byte = np.frexp(amax)[1] - 1 + 127 - (7 if fmt == "e4m3" else 14)
    else:
        mant, ex = np.frexp(amax / 6.0)
        byte = np.where(mant > 0.5, ex, ex - 1) + 127
    byte = np.clip(np.where(amax > 0, byte, 1), 1, 254)
    scaled = (w * np.exp2(127.0 - byte)[:, None, :]).reshape(k, n).astype(np.float32)
    by_word = np.ascontiguousarray(scaled.reshape(k // 512, 128, 4, n).transpose(0, 1, 3, 2))
    if fmt in ("e4m3", "e5m2"):
        words = by_word.astype(ml_dtypes.float8_e4m3fn if fmt == "e4m3" else ml_dtypes.float8_e5m2).view(np.uint8)
    else:
        c = by_word.astype(ml_dtypes.float4_e2m1fn).view(np.uint8) & 0xF
        words = (c[..., 0::2] | (c[..., 1::2] << 4)).reshape(k // 512, 128, 2 * n)
    return np.ascontiguousarray(words), np.ascontiguousarray(byte.astype(np.uint8).reshape(k // 512, 16, n))


def unpack_weight(words, scales, fmt):
    g, _, n = scales.shape
    words = np.ascontiguousarray(words).reshape(g, 128, n, -1)
    if fmt in ("e4m3", "e5m2"):
        vals = words.view(ml_dtypes.float8_e4m3fn if fmt == "e4m3" else ml_dtypes.float8_e5m2).astype(np.float64)
    else:
        nib = np.empty((g, 128, n, 4), np.uint8)
        nib[..., 0::2] = words & 0xF
        nib[..., 1::2] = words >> 4
        vals = E2M1[nib]
    vals = vals * np.repeat(np.exp2(scales.astype(np.float64) - 127.0), 8, axis=1)[..., None]
    return vals.transpose(0, 1, 3, 2).reshape(g * 512, n)


K, T, I, J, N, Z, S, V, O = 512, 1024, 512, 256, 256, 1024, 1024, 1024, 128


def setup_inputs():
    n = np.random.standard_normal
    idx = np.random.permutation(T)[:I]
    idx2 = np.random.permutation(Z)[:J]
    idx3 = np.random.permutation(V)[:J]
    idx4 = np.random.permutation(J)[:O]
    idx5 = np.random.permutation(J)[:O]
    idx6 = np.random.permutation(S)[:N]
    fk = mx_kscale(K)
    fi = mx_kscale(I)
    ti = np.ones(T)
    ti[idx] = fi
    xkp = pack_weight(n((K, T)) * 0.3 * fk[:, None] * ti, "e2m1")
    xqp = pack_weight(n((K, Z)) * 0.3 / fk[:, None], "e4m3")
    xrp = pack_weight(n((K, V)) * 0.3 / fk[:, None], "e5m2")
    vsp = pack_weight(n((I, S)) / fi[:, None], "e4m3")
    return {
        "xk_words": xkp[0],
        "xk_scales": xkp[1],
        "xq_words": xqp[0],
        "xq_scales": xqp[1],
        "xr_words": xrp[0],
        "xr_scales": xrp[1],
        "vs_words": vsp[0],
        "vs_scales": vsp[1],
        "offs": striped(idx),
        "offs2": striped(idx2),
        "offs3": striped(idx3),
        "offs4": striped(idx4),
        "offs5": striped(idx5),
        "offs6": striped(idx6),
    }


def reference(xk_words, xk_scales, xq_words, xq_scales, xr_words, xr_scales, vs_words, vs_scales, offs, offs2, offs3, offs4, offs5, offs6):
    idx = unstriped(offs)
    idx2 = unstriped(offs2)
    idx3 = unstriped(offs3)
    idx4 = unstriped(offs4)
    idx5 = unstriped(offs5)
    idx6 = unstriped(offs6)
    xku = unpack_weight(xk_words, xk_scales, "e2m1")
    xqu = unpack_weight(xq_words, xq_scales, "e4m3")
    xru = unpack_weight(xr_words, xr_scales, "e5m2")
    vsu = unpack_weight(vs_words, vs_scales, "e4m3")
    xkidxg = xku[:, idx]
    xqidx2g = xqu[:, idx2]
    s1 = xkidxg.T @ xqidx2g
    xridx3g = xru[:, idx3]
    s2 = xkidxg.T @ xridx3g
    hid = np.abs(s1[:, idx4] - s2[:, idx5])
    vsidx6g = vsu[:, idx6]
    hidq = mxq(hid, 0, "e5m2")
    y = vsidx6g.T @ hidq
    return y

@@ -1,0 +1,146 @@
+from contextlib import ExitStack
+
+import concourse.mybir as mybir
+
+K, T, I, J, N, O = 512, 1024, 512, 256, 256, 128
+FLOPS = 2 * K * I * J * 2 + 2 * I * N * O
+
+F32 = mybir.dt.float32
+BF16 = mybir.dt.bfloat16
+I32 = mybir.dt.int32
+U32 = mybir.dt.uint32
+U16 = mybir.dt.uint16
+U8 = mybir.dt.uint8
+E2M1 = mybir.dt.float4_e2m1fn_x4
+E4M3 = mybir.dt.float8_e4m3fn_x4
+E5M2 = mybir.dt.float8_e5m2_x4
+ACT = mybir.ActivationFunctionType
+ALU = mybir.AluOpType
+
+P = 128
+PACK = 4
+ALIGN = 64
+
+
+def tile_list_contest_rivals_looked_plain_kernel(
+    tc, xk_words, xk_scales, xq_words, xq_scales, xr_words, xr_scales, vs_words, vs_scales,
+    offs, offs2, offs3, offs4, offs5, offs6, out,
+):
+    nc = tc.nc
+    with ExitStack() as ctx:
+        lists = ctx.enter_context(tc.tile_pool(name="lists", bufs=1))
+        sb = ctx.enter_context(tc.tile_pool(name="sb", bufs=1))
+        psum = ctx.enter_context(tc.psum_pool(name="psum", bufs=1))
+
+        def load_list(src, name):
+            tile = lists.tile(list(src.shape), U16, name=name)
+            nc.sync.dma_start(tile[:], src)
+            return tile
+
+        def load_words(src, dtype, name):
+            tile = sb.tile([P, T], dtype, name=name, align_bytes=ALIGN)
+            nc.sync.dma_start(tile[:].bitcast(I32), src.bitcast(I32))
+            return tile
+
+        def zero_scales(name):
+            tile = sb.tile([P, T], U8, name=name, align_bytes=ALIGN)
+            nc.vector.memset(tile[:].bitcast(I32), 0)
+            return tile
+
+        def load_scales(tile, src, queue):
+            for q in range(4):
+                queue.dma_start(tile[32 * q : 32 * q + 4, :].bitcast(I32), src[0, 4 * q : 4 * q + 4, :].bitcast(I32))
+
+        def gather(window, offsets, count, dtype, name):
+            tile = sb.tile([P, count], dtype, name=name, align_bytes=ALIGN)
+            nc.vector.tensor_copy(tile[:], window[:].indirect(offsets[:]))
+            return tile
+
+        def words8(src):
+            return src[0].rearrange("p c r -> p (c r)")
+
+        k_sc = zero_scales("k_sc")
+        q_sc = zero_scales("q_sc")
+        r_sc = zero_scales("r_sc")
+        v_sc = zero_scales("v_sc")
+
+        l1 = load_list(offs, "l1")
+        k_w = load_words(xk_words[0], U16, "k_w")
+        load_scales(k_sc, xk_scales, nc.scalar)
+        l2 = load_list(offs2, "l2")
+        q_w = load_words(words8(xq_words), U32, "q_w")
+        load_scales(q_sc, xq_scales, nc.sync)
+        l3 = load_list(offs3, "l3")
+        r_w = load_words(words8(xr_words), U32, "r_w")
+        load_scales(r_sc, xr_scales, nc.sync)
+        l4 = load_list(offs4, "l4")
+        l6 = load_list(offs6, "l6")
+        v_w = load_words(words8(vs_words), U32, "v_w")
+        l5 = load_list(offs5, "l5")
+        load_scales(v_sc, vs_scales, nc.sync)
+
+        kg_list = gather(k_w, l1, I, U16, "kg_list")
+        kg_sc = sb.tile([P, I], U8, name="kg_sc", align_bytes=ALIGN)
+        nc.vector.tensor_copy(kg_sc[:].rearrange("p (t m) -> p m t", t=PACK), k_sc[:].indirect(l1[:]))
+        kg_w = sb.tile([P, I], U16, name="kg_w", align_bytes=ALIGN)
+        nc.vector.tensor_copy(
+            kg_w[:].rearrange("p (t m) -> p t m", t=PACK), kg_list[:].rearrange("p (m t) -> p t m", t=PACK)
+        )
+        qg_w = gather(q_w, l2, J, U32, "qg_w")
+        qg_sc = gather(q_sc, l2, J, U8, "qg_sc")
+        rg_w = gather(r_w, l3, J, U32, "rg_w")
+        rg_sc = gather(r_sc, l3, J, U8, "rg_sc")
+
+        def scores(t, words, scales, fmt, name):
+            bank = psum.tile([P, J], F32, name=name, tag=name)
+            cols = slice(t * P, (t + 1) * P)
+            nc.tensor.matmul_mx(
+                out=bank[:], lhsT=kg_w[:, cols].bitcast(E2M1), lhsT_scale=kg_sc[:, cols],
+                rhs=words[:].bitcast(fmt), rhs_scale=scales[:], start=True, stop=True,
+            )
+            return bank
+
+        s1_ps = [scores(t, qg_w, qg_sc, E4M3, "bank%d" % t) for t in range(PACK)]
+        s2_ps = [scores(t, rg_w, rg_sc, E5M2, "bank%d" % (PACK + t)) for t in range(PACK)]
+
+        s1 = [sb.tile([P, J], F32, name="s1_%d" % t) for t in range(PACK)]
+        s2 = [sb.tile([P, J], F32, name="s2_%d" % t) for t in range(PACK)]
+        g1 = [sb.tile([P, O], F32, name="g1_%d" % t) for t in range(PACK)]
+        diff = sb.tile([P, PACK, O], F32, name="diff")
+
+        for t in range(PACK):
+            nc.scalar.activation(s1[t][:], s1_ps[t][:], ACT.Copy)
+
+        vg_w = gather(v_w, l6, N, U32, "vg_w")
+        vg_sc = gather(v_sc, l6, N, U8, "vg_sc")
+
+        for t in range(PACK):
+            nc.scalar.activation(g1[t][:], s1[t][:].indirect(l4[:]), ACT.Copy)
+            if t == 0:
+                nc.vector.tensor_copy(s2[t][:], s2_ps[t][:])
+            else:
+                nc.scalar.activation(s2[t][:], s2_ps[t][:], ACT.Copy)
+            nc.vector.tensor_tensor(diff[:, t, :], s2[t][:].indirect(l5[:]), g1[t][:], ALU.subtract)
+
+        hid = sb.tile([P, O * PACK], BF16, name="hid", align_bytes=ALIGN)
+        nc.scalar.activation(
+            hid[:].rearrange("p (o t) -> p o t", t=PACK), diff[:].rearrange("p t o -> p o t"), ACT.Abs
+        )
+        hq_w = sb.tile([P, O], U32, name="hq_w", align_bytes=ALIGN)
+        hq_sc = sb.tile([P, O], U8, name="hq_sc", align_bytes=ALIGN)
+        nc.vector.quantize_mx(out=hq_w[:].bitcast(E5M2), scales=hq_sc[:], in_=hid[:])
+
+        for h in range(N // P):
+            cols = slice(h * P, (h + 1) * P)
+            bank = psum.tile([P, O], F32, name="y%d" % h, tag="bank%d" % h)
+            nc.tensor.matmul_mx(
+                out=bank[:], lhsT=vg_w[:, cols].bitcast(E4M3), lhsT_scale=vg_sc[:, cols],
+                rhs=hq_w[:].bitcast(E5M2), rhs_scale=hq_sc[:], start=True, stop=True,
+            )
+            y = sb.tile([P, O], F32, name="y_sb%d" % h)
+            if h == 0:
+                nc.vector.tensor_copy(y[:], bank[:])
+                nc.sync.dma_start(out[cols, :], y[:])
+            else:
+                nc.scalar.activation(y[:], bank[:], ACT.Copy)
+                nc.scalar.dma_start(out[cols, :], y[:])

@@ -37,18 +37,18 @@ def tile_list_contest_rivals_looked_plain_kernel(
             nc.sync.dma_start(tile[:], src)
             return tile
 
-        def load_words(src, dtype, name):
+        def load_words(src, dtype, name, queue):
             tile = sb.tile([P, T], dtype, name=name, align_bytes=ALIGN)
-            nc.sync.dma_start(tile[:].bitcast(I32), src.bitcast(I32))
+            queue.dma_start(tile[:].bitcast(I32), src.bitcast(I32))
             return tile
 
-        def zero_scales(name):
+        def zero_scales(name, engine):
             tile = sb.tile([P, T], U8, name=name, align_bytes=ALIGN)
-            nc.vector.memset(tile[:].bitcast(I32), 0)
+            engine.memset(tile[:].bitcast(I32), 0)
             return tile
 
-        def load_scales(tile, src, queue):
-            for q in range(4):
+        def load_scales(tile, src, queue, quadrants):
+            for q in quadrants:
                 queue.dma_start(tile[32 * q : 32 * q + 4, :].bitcast(I32), src[0, 4 * q : 4 * q + 4, :].bitcast(I32))
 
         def gather(window, offsets, count, dtype, name):
@@ -59,25 +59,29 @@ def tile_list_contest_rivals_looked_plain_kernel(
         def words8(src):
             return src[0].rearrange("p c r -> p (c r)")
 
-        k_sc = zero_scales("k_sc")
-        q_sc = zero_scales("q_sc")
-        r_sc = zero_scales("r_sc")
-        v_sc = zero_scales("v_sc")
+        k_sc = zero_scales("k_sc", nc.vector)
+        q_sc = zero_scales("q_sc", nc.vector)
+        r_sc = zero_scales("r_sc", nc.vector)
+        v_sc = zero_scales("v_sc", nc.vector)
 
         l1 = load_list(offs, "l1")
-        k_w = load_words(xk_words[0], U16, "k_w")
-        load_scales(k_sc, xk_scales, nc.scalar)
+        k_w = load_words(xk_words[0], U16, "k_w", nc.sync)
+        load_scales(k_sc, xk_scales, nc.scalar, range(2))
+        load_scales(k_sc, xk_scales, nc.sync, range(2, 4))
+        load_scales(q_sc, xq_scales, nc.scalar, range(4))
+        q_w = load_words(words8(xq_words), U32, "q_w", nc.sync)
         l2 = load_list(offs2, "l2")
-        q_w = load_words(words8(xq_words), U32, "q_w")
-        load_scales(q_sc, xq_scales, nc.sync)
+        load_scales(r_sc, xr_scales, nc.scalar, range(1))
         l3 = load_list(offs3, "l3")
-        r_w = load_words(words8(xr_words), U32, "r_w")
-        load_scales(r_sc, xr_scales, nc.sync)
+        r_w = load_words(words8(xr_words), U32, "r_w", nc.sync)
+        v_w = load_words(words8(vs_words), U32, "v_w", nc.sync)
+        load_scales(r_sc, xr_scales, nc.sync, range(1, 3))
         l4 = load_list(offs4, "l4")
+        load_scales(r_sc, xr_scales, nc.sync, range(3, 4))
         l6 = load_list(offs6, "l6")
-        v_w = load_words(words8(vs_words), U32, "v_w")
+        load_scales(v_sc, vs_scales, nc.sync, range(2))
         l5 = load_list(offs5, "l5")
-        load_scales(v_sc, vs_scales, nc.sync)
+        load_scales(v_sc, vs_scales, nc.sync, range(2, 4))
 
         kg_list = gather(k_w, l1, I, U16, "kg_list")
         kg_sc = sb.tile([P, I], U8, name="kg_sc", align_bytes=ALIGN)
@@ -112,20 +116,26 @@ def tile_list_contest_rivals_looked_plain_kernel(
             nc.scalar.activation(s1[t][:], s1_ps[t][:], ACT.Copy)
 
         vg_w = gather(v_w, l6, N, U32, "vg_w")
-        vg_sc = gather(v_sc, l6, N, U8, "vg_sc")
 
         for t in range(PACK):
             nc.scalar.activation(g1[t][:], s1[t][:].indirect(l4[:]), ACT.Copy)
-            if t == 0:
+        for t in range(PACK):
+            if t < 2:
                 nc.vector.tensor_copy(s2[t][:], s2_ps[t][:])
             else:
                 nc.scalar.activation(s2[t][:], s2_ps[t][:], ACT.Copy)
+        for t in range(PACK):
             nc.vector.tensor_tensor(diff[:, t, :], s2[t][:].indirect(l5[:]), g1[t][:], ALU.subtract)
 
+        vg_sc = gather(v_sc, l6, N, U8, "vg_sc")
+
         hid = sb.tile([P, O * PACK], BF16, name="hid", align_bytes=ALIGN)
-        nc.scalar.activation(
-            hid[:].rearrange("p (o t) -> p o t", t=PACK), diff[:].rearrange("p t o -> p o t"), ACT.Abs
-        )
+        for t in range(0, PACK, 2):
+            nc.scalar.activation(
+                hid[:].rearrange("p (o t) -> p o t", t=PACK)[:, :, t : t + 2],
+                diff[:, t : t + 2, :].rearrange("p t o -> p o t"),
+                ACT.Abs,
+            )
         hq_w = sb.tile([P, O], U32, name="hq_w", align_bytes=ALIGN)
         hq_sc = sb.tile([P, O], U8, name="hq_sc", align_bytes=ALIGN)
         nc.vector.quantize_mx(out=hq_w[:].bitcast(E5M2), scales=hq_sc[:], in_=hid[:])

@@ -30,6 +30,7 @@ def tile_list_contest_rivals_looked_plain_kernel(
     with ExitStack() as ctx:
         lists = ctx.enter_context(tc.tile_pool(name="lists", bufs=1))
         sb = ctx.enter_context(tc.tile_pool(name="sb", bufs=1))
+        shared = ctx.enter_context(tc.tile_pool(name="shared", bufs=1))
         psum = ctx.enter_context(tc.psum_pool(name="psum", bufs=1))
 
         def load_list(src, name):
@@ -37,8 +38,7 @@ def tile_list_contest_rivals_looked_plain_kernel(
             nc.sync.dma_start(tile[:], src)
             return tile
 
-        def load_words(src, dtype, name, queue):
-            tile = sb.tile([P, T], dtype, name=name, align_bytes=ALIGN)
+        def load_words(src, tile, queue):
             queue.dma_start(tile[:].bitcast(I32), src.bitcast(I32))
             return tile
 
@@ -65,33 +65,36 @@ def tile_list_contest_rivals_looked_plain_kernel(
         v_sc = zero_scales("v_sc", nc.vector)
 
         l1 = load_list(offs, "l1")
-        k_w = load_words(xk_words[0], U16, "k_w", nc.sync)
+        k_w = load_words(xk_words[0], sb.tile([P, T], U16, name="k_w", align_bytes=ALIGN), nc.scalar)
         load_scales(k_sc, xk_scales, nc.scalar, range(2))
         load_scales(k_sc, xk_scales, nc.sync, range(2, 4))
-        load_scales(q_sc, xq_scales, nc.scalar, range(4))
-        q_w = load_words(words8(xq_words), U32, "q_w", nc.sync)
+        q_w = load_words(words8(xq_words), shared.tile([P, T], U32, name="q_w", align_bytes=ALIGN, offset=0), nc.sync)
+        load_scales(q_sc, xq_scales, nc.scalar, range(3))
+        load_scales(q_sc, xq_scales, nc.sync, range(3, 4))
         l2 = load_list(offs2, "l2")
         load_scales(r_sc, xr_scales, nc.scalar, range(1))
+        r_w = load_words(words8(xr_words), sb.tile([P, T], U32, name="r_w", align_bytes=ALIGN), nc.sync)
         l3 = load_list(offs3, "l3")
-        r_w = load_words(words8(xr_words), U32, "r_w", nc.sync)
-        v_w = load_words(words8(vs_words), U32, "v_w", nc.sync)
-        load_scales(r_sc, xr_scales, nc.sync, range(1, 3))
+        load_scales(r_sc, xr_scales, nc.sync, range(1, 4))
         l4 = load_list(offs4, "l4")
-        load_scales(r_sc, xr_scales, nc.sync, range(3, 4))
+        v_w = load_words(words8(vs_words), shared.tile([P, T], U32, name="v_w", align_bytes=ALIGN, offset=4 * T), nc.sync)
         l6 = load_list(offs6, "l6")
         load_scales(v_sc, vs_scales, nc.sync, range(2))
         l5 = load_list(offs5, "l5")
         load_scales(v_sc, vs_scales, nc.sync, range(2, 4))
 
-        kg_list = gather(k_w, l1, I, U16, "kg_list")
-        kg_sc = sb.tile([P, I], U8, name="kg_sc", align_bytes=ALIGN)
-        nc.vector.tensor_copy(kg_sc[:].rearrange("p (t m) -> p m t", t=PACK), k_sc[:].indirect(l1[:]))
-        kg_w = sb.tile([P, I], U16, name="kg_w", align_bytes=ALIGN)
-        nc.vector.tensor_copy(
-            kg_w[:].rearrange("p (t m) -> p t m", t=PACK), kg_list[:].rearrange("p (m t) -> p t m", t=PACK)
-        )
+        kl_w = gather(k_w, l1, I, U16, "kl_w")
+        kl_sc = gather(k_sc, l1, I, U8, "kl_sc")
         qg_w = gather(q_w, l2, J, U32, "qg_w")
         qg_sc = gather(q_sc, l2, J, U8, "qg_sc")
+        kg_w = shared.tile([P, I], U16, name="kg_w", align_bytes=ALIGN, offset=0)
+        kg_sc = shared.tile([P, I], U8, name="kg_sc", align_bytes=ALIGN, offset=2 * I)
+        for ts in (slice(0, 2), slice(2, PACK)):
+            for dealt, listed, run in ((kg_w, kl_w, 8), (kg_sc, kl_sc, 16)):
+                nc.vector.tensor_copy(
+                    dealt[:].rearrange("p (t c m) -> p c t m", t=PACK, m=run)[:, :, ts, :],
+                    listed[:].rearrange("p (c m t) -> p c t m", t=PACK, m=run)[:, :, ts, :],
+                )
         rg_w = gather(r_w, l3, J, U32, "rg_w")
         rg_sc = gather(r_sc, l3, J, U8, "rg_sc")
 
@@ -108,7 +111,8 @@ def tile_list_contest_rivals_looked_plain_kernel(
         s2_ps = [scores(t, rg_w, rg_sc, E5M2, "bank%d" % (PACK + t)) for t in range(PACK)]
 
         s1 = [sb.tile([P, J], F32, name="s1_%d" % t) for t in range(PACK)]
-        s2 = [sb.tile([P, J], F32, name="s2_%d" % t) for t in range(PACK)]
+        s2 = [shared.tile([P, J], F32, name="s2_%d" % t, offset=4 * T + 4 * J * t) for t in range(2)]
+        s2 = s2 + [sb.tile([P, J], F32, name="s2_%d" % t) for t in range(2, PACK)]
         g1 = [sb.tile([P, O], F32, name="g1_%d" % t) for t in range(PACK)]
         diff = sb.tile([P, PACK, O], F32, name="diff")
 

from contextlib import ExitStack

import concourse.mybir as mybir

K, T, I, J, N, O = 512, 1024, 512, 256, 256, 128
FLOPS = 2 * K * I * J * 2 + 2 * I * N * O

F32 = mybir.dt.float32
BF16 = mybir.dt.bfloat16
I32 = mybir.dt.int32
U32 = mybir.dt.uint32
U16 = mybir.dt.uint16
U8 = mybir.dt.uint8
E2M1 = mybir.dt.float4_e2m1fn_x4
E4M3 = mybir.dt.float8_e4m3fn_x4
E5M2 = mybir.dt.float8_e5m2_x4
ACT = mybir.ActivationFunctionType
ALU = mybir.AluOpType

P = 128
PACK = 4
ALIGN = 64


def tile_list_contest_rivals_looked_plain_kernel(
    tc, xk_words, xk_scales, xq_words, xq_scales, xr_words, xr_scales, vs_words, vs_scales,
    offs, offs2, offs3, offs4, offs5, offs6, out,
):
    nc = tc.nc
    with ExitStack() as ctx:
        lists = ctx.enter_context(tc.tile_pool(name="lists", bufs=1))
        sb = ctx.enter_context(tc.tile_pool(name="sb", bufs=1))
        shared = ctx.enter_context(tc.tile_pool(name="shared", bufs=1))
        psum = ctx.enter_context(tc.psum_pool(name="psum", bufs=1))

        def load_list(src, name):
            tile = lists.tile(list(src.shape), U16, name=name)
            nc.sync.dma_start(tile[:], src)
            return tile

        def load_words(src, tile, queue):
            queue.dma_start(tile[:].bitcast(I32), src.bitcast(I32))
            return tile

        def zero_scales(name, engine):
            tile = sb.tile([P, T], U8, name=name, align_bytes=ALIGN)
            engine.memset(tile[:].bitcast(I32), 0)
            return tile

        def load_scales(tile, src, queue, quadrants):
            for q in quadrants:
                queue.dma_start(tile[32 * q : 32 * q + 4, :].bitcast(I32), src[0, 4 * q : 4 * q + 4, :].bitcast(I32))

        def gather(window, offsets, count, dtype, name):
            tile = sb.tile([P, count], dtype, name=name, align_bytes=ALIGN)
            nc.vector.tensor_copy(tile[:], window[:].indirect(offsets[:]))
            return tile

        def words8(src):
            return src[0].rearrange("p c r -> p (c r)")

        k_sc = zero_scales("k_sc", nc.vector)
        q_sc = zero_scales("q_sc", nc.vector)
        r_sc = zero_scales("r_sc", nc.vector)
        v_sc = zero_scales("v_sc", nc.vector)

        l1 = load_list(offs, "l1")
        k_w = load_words(xk_words[0], sb.tile([P, T], U16, name="k_w", align_bytes=ALIGN), nc.scalar)
        load_scales(k_sc, xk_scales, nc.scalar, range(2))
        load_scales(k_sc, xk_scales, nc.sync, range(2, 4))
        q_w = load_words(words8(xq_words), shared.tile([P, T], U32, name="q_w", align_bytes=ALIGN, offset=0), nc.sync)
        load_scales(q_sc, xq_scales, nc.scalar, range(3))
        load_scales(q_sc, xq_scales, nc.sync, range(3, 4))
        l2 = load_list(offs2, "l2")
        load_scales(r_sc, xr_scales, nc.scalar, range(1))
        r_w = load_words(words8(xr_words), sb.tile([P, T], U32, name="r_w", align_bytes=ALIGN), nc.sync)
        l3 = load_list(offs3, "l3")
        load_scales(r_sc, xr_scales, nc.sync, range(1, 4))
        l4 = load_list(offs4, "l4")
        v_w = load_words(words8(vs_words), shared.tile([P, T], U32, name="v_w", align_bytes=ALIGN, offset=4 * T), nc.sync)
        l6 = load_list(offs6, "l6")
        load_scales(v_sc, vs_scales, nc.sync, range(2))
        l5 = load_list(offs5, "l5")
        load_scales(v_sc, vs_scales, nc.sync, range(2, 4))

        kl_w = gather(k_w, l1, I, U16, "kl_w")
        kl_sc = gather(k_sc, l1, I, U8, "kl_sc")
        qg_w = gather(q_w, l2, J, U32, "qg_w")
        qg_sc = gather(q_sc, l2, J, U8, "qg_sc")
        kg_w = shared.tile([P, I], U16, name="kg_w", align_bytes=ALIGN, offset=0)
        kg_sc = shared.tile([P, I], U8, name="kg_sc", align_bytes=ALIGN, offset=2 * I)
        for ts in (slice(0, 2), slice(2, PACK)):
            for dealt, listed, run in ((kg_w, kl_w, 8), (kg_sc, kl_sc, 16)):
                nc.vector.tensor_copy(
                    dealt[:].rearrange("p (t c m) -> p c t m", t=PACK, m=run)[:, :, ts, :],
                    listed[:].rearrange("p (c m t) -> p c t m", t=PACK, m=run)[:, :, ts, :],
                )
        rg_w = gather(r_w, l3, J, U32, "rg_w")
        rg_sc = gather(r_sc, l3, J, U8, "rg_sc")

        def scores(t, words, scales, fmt, name):
            bank = psum.tile([P, J], F32, name=name, tag=name)
            cols = slice(t * P, (t + 1) * P)
            nc.tensor.matmul_mx(
                out=bank[:], lhsT=kg_w[:, cols].bitcast(E2M1), lhsT_scale=kg_sc[:, cols],
                rhs=words[:].bitcast(fmt), rhs_scale=scales[:], start=True, stop=True,
            )
            return bank

        s1_ps = [scores(t, qg_w, qg_sc, E4M3, "bank%d" % t) for t in range(PACK)]
        s2_ps = [scores(t, rg_w, rg_sc, E5M2, "bank%d" % (PACK + t)) for t in range(PACK)]

        s1 = [sb.tile([P, J], F32, name="s1_%d" % t) for t in range(PACK)]
        s2 = [shared.tile([P, J], F32, name="s2_%d" % t, offset=4 * T + 4 * J * t) for t in range(2)]
        s2 = s2 + [sb.tile([P, J], F32, name="s2_%d" % t) for t in range(2, PACK)]
        g1 = [sb.tile([P, O], F32, name="g1_%d" % t) for t in range(PACK)]
        diff = sb.tile([P, PACK, O], F32, name="diff")

        for t in range(PACK):
            nc.scalar.activation(s1[t][:], s1_ps[t][:], ACT.Copy)

        vg_w = gather(v_w, l6, N, U32, "vg_w")

        for t in range(PACK):
            nc.scalar.activation(g1[t][:], s1[t][:].indirect(l4[:]), ACT.Copy)
        for t in range(PACK):
            if t < 2:
                nc.vector.tensor_copy(s2[t][:], s2_ps[t][:])
            else:
                nc.scalar.activation(s2[t][:], s2_ps[t][:], ACT.Copy)
        for t in range(PACK):
            nc.vector.tensor_tensor(diff[:, t, :], s2[t][:].indirect(l5[:]), g1[t][:], ALU.subtract)

        vg_sc = gather(v_sc, l6, N, U8, "vg_sc")

        hid = sb.tile([P, O * PACK], BF16, name="hid", align_bytes=ALIGN)
        for t in range(0, PACK, 2):
            nc.scalar.activation(
                hid[:].rearrange("p (o t) -> p o t", t=PACK)[:, :, t : t + 2],
                diff[:, t : t + 2, :].rearrange("p t o -> p o t"),
                ACT.Abs,
            )
        hq_w = sb.tile([P, O], U32, name="hq_w", align_bytes=ALIGN)
        hq_sc = sb.tile([P, O], U8, name="hq_sc", align_bytes=ALIGN)
        nc.vector.quantize_mx(out=hq_w[:].bitcast(E5M2), scales=hq_sc[:], in_=hid[:])

        for h in range(N // P):
            cols = slice(h * P, (h + 1) * P)
            bank = psum.tile([P, O], F32, name="y%d" % h, tag="bank%d" % h)
            nc.tensor.matmul_mx(
                out=bank[:], lhsT=vg_w[:, cols].bitcast(E4M3), lhsT_scale=vg_sc[:, cols],
                rhs=hq_w[:].bitcast(E5M2), rhs_scale=hq_sc[:], start=True, stop=True,
            )
            y = sb.tile([P, O], F32, name="y_sb%d" % h)
            if h == 0:
                nc.vector.tensor_copy(y[:], bank[:])
                nc.sync.dma_start(out[cols, :], y[:])
            else:
                nc.scalar.activation(y[:], bank[:], ACT.Copy)
                nc.scalar.dma_start(out[cols, :], y[:])
